import numpy as np
import ml_dtypes


def mxq(x, axis, fmt="e4m3"):
    dtype, down = {"e4m3": (ml_dtypes.float8_e4m3fn, 7), "e5m2": (ml_dtypes.float8_e5m2, 14)}[fmt]
    v = np.moveaxis(np.asarray(x, np.float32).astype(ml_dtypes.bfloat16).astype(np.float64), axis, -1)
    blocks = v.reshape(v.shape[:-1] + (-1, 32))
    amax = np.abs(blocks).max(-1, keepdims=True)
    byte = np.maximum(np.where(amax > 0, np.frexp(amax)[1] - 1 + 127, 0) - down, 1)
    scale = np.exp2(byte - 127.0)
    codes = (blocks / scale).astype(np.float32).astype(dtype).astype(np.float64)
    return np.moveaxis((codes * scale).reshape(v.shape), -1, axis)


WIDE = False


def mx_kscale(k):
    if not WIDE:
        return np.ones(k)
    levels = np.array([10, -10, 5, -5, 0])
    if k % 512:
        return np.exp2(np.random.permutation(np.resize(levels, k // 32))).repeat(32)
    a = np.empty((k // 512, 16))
    for p in range(k // 512):
        a[p, :8] = np.random.permutation(np.resize(levels, 8))
        for g in range(8):
            far = levels[np.abs(levels - a[p, g]) >= 10]
            a[p, g + 8] = far[np.random.randint(len(far))]
    return np.exp2(a.ravel()).repeat(32)


def f64(x):
    return np.asarray(x).astype(np.float64)


def striped(idx):
    return np.tile(idx.reshape(-1, 16).T, (8, 1)).astype(np.uint16)


def unstriped(offs):
    return offs[:16].T.reshape(-1).astype(np.int64)


E2M1 = np.array([0.0, 0.5, 1.0, 1.5, 2.0, 3.0, 4.0, 6.0, -0.0, -0.5, -1.0, -1.5, -2.0, -3.0, -4.0, -6.0])


def pack_weight(w, fmt):
    k, n = w.shape
    w = f64(np.asarray(w, np.float32).astype(ml_dtypes.bfloat16)).reshape(k // 32, 32, n)
    amax = np.abs(w).max(1)
    if fmt == "e4m3":
        byte = np.frexp(amax)[1] - 1 + 127 - 7
    else:
        mant, ex = np.frexp(amax / 6.0)
        byte = np.where(mant > 0.5, ex, ex - 1) + 127
    byte = np.clip(np.where(amax > 0, byte, 1), 1, 254)
    scaled = (w * np.exp2(127.0 - byte)[:, None, :]).reshape(k, n).astype(np.float32)
    by_word = np.ascontiguousarray(scaled.reshape(k // 512, 128, 4, n).transpose(0, 1, 3, 2))
    if fmt == "e4m3":
        words = by_word.astype(ml_dtypes.float8_e4m3fn).view(np.uint8)
    else:
        c = by_word.astype(ml_dtypes.float4_e2m1fn).view(np.uint8) & 0xF
        words = (c[..., 0::2] | (c[..., 1::2] << 4)).reshape(k // 512, 128, 2 * n)
    return np.ascontiguousarray(words), np.ascontiguousarray(byte.astype(np.uint8).reshape(k // 512, 16, n))


def unpack_weight(words, scales, fmt):
    g, _, n = scales.shape
    words = np.ascontiguousarray(words).reshape(g, 128, n, -1)
    if fmt == "e4m3":
        vals = words.view(ml_dtypes.float8_e4m3fn).astype(np.float64)
    else:
        nib = np.empty((g, 128, n, 4), np.uint8)
        nib[..., 0::2] = words & 0xF
        nib[..., 1::2] = words >> 4
        vals = E2M1[nib]
    vals = vals * np.repeat(np.exp2(scales.astype(np.float64) - 127.0), 8, axis=1)[..., None]
    return vals.transpose(0, 1, 3, 2).reshape(g * 512, n)


def gelu(v):
    return 0.5 * v * (1.0 + np.tanh(np.sqrt(2.0 / np.pi) * (v + 0.044715 * v**3)))


def bf(x):
    return np.asarray(x, np.float32).astype(ml_dtypes.bfloat16)


def planes(Y):
    n, m = Y.shape
    b = f64(bf(Y)).reshape(n // 32, 32, m)
    amax = np.abs(b).max(1)
    byte = np.clip(np.where(amax > 0, np.frexp(amax)[1] - 1 + 127 - 7, 1), 1, 254)
    codes = (b * np.exp2(127.0 - byte)[:, None, :]).reshape(n, m).astype(np.float32).astype(ml_dtypes.float8_e4m3fn).view(np.uint8)
    words = codes.reshape(n // 512, 128, 4, m).transpose(0, 1, 3, 2)
    return np.ascontiguousarray(words), np.ascontiguousarray(byte.astype(np.uint8).reshape(n // 512, 16, m))


K, T, S, H, T2, P, N = 1024, 4096, 1024, 512, 2048, 1024, 768


def setup_inputs():
    n = np.random.standard_normal
    s, u = mx_kscale(K)[:, None], mx_kscale(H)[:, None]
    d = {}
    d["tab_words"], d["tab_scales"] = pack_weight(n((K, T)) * s, "e4m3")
    d["offs"] = striped(np.random.permutation(T)[:S])
    d["offs2"] = striped(np.random.permutation(T2)[:S])
    d["offs3"] = striped(np.random.permutation(T2)[:P])
    d["w1"] = (n((K, H)) / s / K ** 0.5).astype(np.float32)
    d["w2_words"], d["w2_scales"] = pack_weight(n((K, H)) / s / K ** 0.5, "e2m1")
    d["gain"] = (np.exp(0.3 * n(H)) * u[:, 0]).astype(np.float32)
    d["wgs"] = np.exp(0.3 * n((128, S))).astype(np.float32)
    d["page0"] = (n((H, T2)) * u).astype(np.float32)
    d["bias"] = (0.5 * n(H) * u[:, 0]).astype(np.float32)
    d["w3"] = (n((H, N)) / u / H ** 0.5).astype(np.float32)
    d["w4_words"], d["w4_scales"] = pack_weight(n((H, N)) / u / H ** 0.5, "e4m3")
    d["delay"] = n((N, P)).astype(np.float32)
    return d


def reference(tab_words, tab_scales, offs, offs2, offs3, w1, w2_words, w2_scales, gain, wgs,
              page0, bias, w3, w4_words, w4_scales, delay):
    v = unpack_weight(tab_words, tab_scales, "e4m3")[:, unstriped(offs)]
    a = mxq(f64(w1), 0, "e4m3").T @ v
    b = unpack_weight(w2_words, w2_scales, "e2m1").T @ v
    h = np.maximum(a, b) * f64(gain)[:, None]
    page = f64(page0).copy()
    page[:, unstriped(offs2)] = np.tile(f64(wgs), (H // 128, 1)) * h
    x = page[:, unstriped(offs3)] + f64(bias)[:, None]
    xq = mxq(x, 0, "e4m3")
    e = mxq(f64(w3), 0, "e4m3").T @ xq
    f = unpack_weight(w4_words, w4_scales, "e4m3").T @ xq
    y = np.abs(e) * f + f64(delay)
    words, scales = planes(page)
    return y, page, words, scales

@@ -1,0 +1,298 @@
+from contextlib import ExitStack
+
+import concourse.mybir as mybir
+from concourse.masks import make_identity
+
+K, T, S, H, T2, PJ, N = 1024, 4096, 1024, 512, 2048, 1024, 768
+FLOPS = 2 * 2 * K * H * S + 2 * 2 * H * N * PJ
+
+F32 = mybir.dt.float32
+BF16 = mybir.dt.bfloat16
+I32 = mybir.dt.int32
+U32 = mybir.dt.uint32
+U16 = mybir.dt.uint16
+U8 = mybir.dt.uint8
+FP8X4 = mybir.dt.float8_e4m3fn_x4
+FP4X4 = mybir.dt.float4_e2m1fn_x4
+ALU = mybir.AluOpType
+ACT = mybir.ActivationFunctionType
+
+P = 128
+PACK = 4
+PASSES = K // (P * PACK)
+BANK = 512
+CHUNK = 256
+NT = N // P
+
+
+def tile_list_blast_hole_charging_kernel(
+    tc, tab_words, tab_scales, offs, offs2, offs3, w1, w2_words, w2_scales, gain, wgs,
+    page0, bias, w3, w4_words, w4_scales, delay, out_0, out_1, out_2, out_3,
+):
+    nc = tc.nc
+    with ExitStack() as ctx:
+        lists = ctx.enter_context(tc.tile_pool(name="lists", bufs=1))
+        keep = ctx.enter_context(tc.tile_pool(name="keep", bufs=1))
+        psum = ctx.enter_context(tc.psum_pool(name="psum", bufs=8))
+
+        def held(name, shape, dtype, tag=None, bufs=1):
+            return keep.tile(shape, dtype, name=name, tag=tag or name, bufs=bufs, align_bytes=64)
+
+        def bank(name, shape):
+            return psum.tile(shape, F32, name=name, tag="bank")
+
+        ts = held("ts", [P, T], U8)
+        nc.vector.memset(ts[:].bitcast(I32), 0)
+        w2s_raw = held("w2s_raw", [P, H], U8)
+        nc.vector.memset(w2s_raw[:].bitcast(I32), 0)
+        tp = held("tp", [P, PASSES, S + H], U8)
+        nc.vector.memset(tp[:].rearrange("p a c -> p (a c)").bitcast(I32), 0)
+        w4s = held("w4s", [P, N], U8)
+        nc.vector.memset(w4s[:].bitcast(I32), 0)
+
+        nc.gpsimd.dma_start(
+            out=ts[0:P:4, :].bitcast(I32), in_=tab_scales.rearrange("a q t -> q a t").bitcast(I32)
+        )
+        nc.gpsimd.dma_start(
+            out=w2s_raw[0:P:4, :].bitcast(I32), in_=w2_scales.rearrange("a q c -> q a c").bitcast(I32)
+        )
+        ident = held("ident", [P, P], F32)
+        make_identity(nc, ident[:])
+
+        offs_t = lists.tile([P, S // 16], U16, name="offs_t")
+        nc.sync.dma_start(offs_t[:], offs)
+        wgs_t = held("wgs_t", [P, S], F32)
+        nc.sync.dma_start(out=wgs_t[:], in_=wgs)
+        gain_t = held("gain_t", [P, PACK], F32)
+        nc.sync.dma_start(out=gain_t[:], in_=gain.rearrange("(p t) -> p t", t=PACK))
+        w2_raw = held("w2_raw", [P, PASSES, 2 * H], U8)
+        nc.sync.dma_start(
+            out=w2_raw[:].bitcast(I32), in_=w2_words.rearrange("a p c -> p a c").bitcast(I32)
+        )
+        w1_raw = []
+        for a in range(PASSES):
+            raw = held(f"w1_raw{a}", [P, PACK, H], F32, tag="w1_raw_y", bufs=2)
+            nc.sync.dma_start(
+                out=raw[:], in_=w1[a * 512 : (a + 1) * 512, :].rearrange("(p j) c -> p j c", j=PACK)
+            )
+            w1_raw.append(raw)
+        tab = []
+        for a in range(PASSES):
+            words = held(f"tab{a}", [P, T], I32, tag=f"tab_delay{a}")
+            nc.sync.dma_start(
+                out=words[:], in_=tab_words[a].rearrange("p t i -> p (t i)").bitcast(I32)
+            )
+            tab.append(words)
+        offs2_t = lists.tile([P, S // 16], U16, name="offs2_t")
+        nc.sync.dma_start(offs2_t[:], offs2)
+        page_rows = page0.rearrange("(p t) m -> p t m", t=PACK)
+        page = [held(f"page{t}", [P, T2], F32) for t in range(PACK)]
+        nc.sync.dma_start(out=page[0][:], in_=page_rows[:, 0, :])
+
+        gs = held("gs", [P, S], U8)
+        nc.vector.tensor_copy(gs[:], ts[:].indirect(offs_t[:]))
+        staged = held("staged", [P, S + H], U8)
+        nc.vector.tensor_copy(
+            staged[:, S:].rearrange("p (t m) -> p m t", t=PACK),
+            w2s_raw[:].rearrange("p (m t) -> p m t", t=PACK),
+        )
+        nc.vector.tensor_copy(staged[:, :S].bitcast(I32), gs[:].bitcast(I32))
+        for q in range(4):
+            nc.gpsimd.dma_start(
+                out=tp[32 * q : 32 * q + 4, :, :].bitcast(I32),
+                in_=staged[32 * q : 32 * q + 32 : 4, :].bitcast(I32),
+            )
+
+        wT = held("wT", [P, S // P, PACK, P], F32, tag="wT_w3")
+        for half in range(2):
+            turned = bank(f"wgsT{half}", [P, 4, P])
+            for b in range(4):
+                jb = 4 * half + b
+                nc.tensor.transpose(turned[:, b, :], wgs_t[:, jb * P : (jb + 1) * P], ident[:])
+            for q in range(4):
+                dst = wT[:, 4 * half : 4 * half + 4, :, 32 * q : 32 * q + 32]
+                src = turned[:].rearrange("j b (p t) -> j b t p", t=PACK)
+                nc.scalar.copy(dst, src)
+        wg = [held(f"wg{h}", [P, PACK, BANK], F32, tag=f"ring{h}") for h in range(2)]
+        for t in range(PACK):
+            for h in range(2):
+                back = bank(f"wgs{t}_{h}", [P, 4, P])
+                for b in range(4):
+                    nc.tensor.transpose(back[:, b, :], wT[:, 4 * h + b, t, :], ident[:])
+                nc.scalar.activation(
+                    wg[h][:, t, :], back[:].rearrange("p b j -> p (b j)"), ACT.Copy,
+                    scale=gain_t[:, t : t + 1],
+                )
+
+        w3_raw = held("w3_raw", [P, PACK, N], F32, tag="wT_w3")
+        nc.sync.dma_start(out=w3_raw[:], in_=w3.rearrange("(p j) c -> p j c", j=PACK))
+        nc.sync.dma_start(out=page[1][:], in_=page_rows[:, 1, :])
+        w4 = held("w4", [P, N], I32)
+        nc.sync.dma_start(out=w4[:], in_=w4_words[0].rearrange("p n i -> p (n i)").bitcast(I32))
+        nc.sync.dma_start(out=page[2][:], in_=page_rows[:, 2, :])
+        nc.sync.dma_start(out=page[3][:], in_=page_rows[:, 3, :])
+        offs3_t = lists.tile([P, PJ // 16], U16, name="offs3_t")
+        nc.sync.dma_start(offs3_t[:], offs3)
+        bias_t = held("bias_t", [P, PACK], F32)
+        nc.sync.dma_start(out=bias_t[:], in_=bias.rearrange("(p t) -> p t", t=PACK))
+        for q in range(4):
+            nc.sync.dma_start(
+                out=w4s[32 * q : 32 * q + 4, :].bitcast(I32),
+                in_=w4_scales[0, 4 * q : 4 * q + 4, :].bitcast(I32),
+            )
+
+        w2d = held("w2d", [P, PASSES, PACK, 2 * P], U8)
+        w1q, w1s = [], []
+        for a in range(PASSES):
+            nc.vector.tensor_copy(
+                w2d[:, a, :, :].rearrange("p t (m b) -> p m t b", b=2),
+                w2_raw[:, a, :].rearrange("p (m t b) -> p m t b", t=PACK, b=2),
+            )
+            grouped = held(f"w1_grouped{a}", [P, PACK * H], BF16, tag=f"grouped{a}")
+            nc.vector.tensor_copy(
+                grouped[:].rearrange("p (t m j) -> p m j t", t=PACK, j=PACK),
+                w1_raw[a][:].rearrange("p j (m t) -> p m j t", t=PACK),
+            )
+            codes = held(f"w1q{a}", [P, H], U32)
+            scales = held(f"w1s{a}", [P, H], U8)
+            nc.vector.quantize_mx(out=codes[:].bitcast(FP8X4), scales=scales[:], in_=grouped[:])
+            w1q.append(codes)
+            w1s.append(scales)
+
+        gw = {}
+        for a in range(PASSES):
+            for h in range(2):
+                gw[a, h] = held(f"gw{a}_{h}", [P, BANK], U32)
+                nc.vector.tensor_copy(
+                    gw[a, h][:], tab[a][:].bitcast(U32).indirect(offs_t[:, 32 * h : 32 * h + 32])
+                )
+
+        delay_rows = delay.rearrange("(b p) j -> p b j", p=P)
+        delay_t = []
+        for h in range(2):
+            rows = held(f"delay{h}", [P, NT, BANK], F32, tag=f"tab_delay{h}")
+            nc.sync.dma_start(out=rows[:], in_=delay_rows[:, :, h * BANK : (h + 1) * BANK])
+            delay_t.append(rows)
+
+        out1_rows = out_1.rearrange("(p t) m -> p t m", t=PACK)
+        pil = [held(f"pil{c}", [P, BANK, PACK], BF16) for c in range(4)]
+
+        def round_page(t, c):
+            nc.scalar.copy(pil[c][:, :, t], page[t][:, c * BANK : (c + 1) * BANK])
+
+        w3q = held("w3q", [P, N], U32)
+        w3s = held("w3s", [P, N], U8)
+        largest = {}
+
+        def first_products(t, h):
+            cols = slice(t * P, (t + 1) * P)
+            acc_a = bank(f"a{t}_{h}", [P, BANK])
+            acc_b = bank(f"b{t}_{h}", [P, BANK])
+            for a in range(PASSES):
+                moving = dict(
+                    rhs=gw[a, h][:].bitcast(FP8X4), rhs_scale=tp[:, a, h * BANK : (h + 1) * BANK],
+                    start=(a == 0), stop=(a == PASSES - 1),
+                )
+                nc.tensor.matmul_mx(
+                    out=acc_a[:], lhsT=w1q[a][:, cols].bitcast(FP8X4), lhsT_scale=w1s[a][:, cols],
+                    **moving,
+                )
+                nc.tensor.matmul_mx(
+                    out=acc_b[:], lhsT=w2d[:, a, t, :].bitcast(FP4X4),
+                    lhsT_scale=tp[:, a, S + t * P : S + (t + 1) * P],
+                    **moving,
+                )
+            a_sb = held(f"a_sb{t}_{h}", [P, BANK], F32, tag="evac", bufs=3)
+            nc.scalar.copy(a_sb[:], acc_a[:])
+            largest[t, h] = held(f"m{t}_{h}", [P, BANK], F32, tag="m_prod", bufs=8)
+            nc.vector.tensor_tensor(largest[t, h][:], acc_b[:], a_sb[:], ALU.max)
+
+        def put(t, h):
+            nc.vector.tensor_tensor(
+                page[t][:].indirect(offs2_t[:, 32 * h : 32 * h + 32]),
+                largest[t, h][:], wg[h][:, t, :], ALU.mult,
+            )
+
+        units = [(t, h) for t in range(PACK) for h in range(2)]
+        first_products(*units[0])
+        for i, (t, h) in enumerate(units):
+            if i + 1 < len(units):
+                first_products(*units[i + 1])
+            put(t, h)
+            if h == 1:
+                nc.sync.dma_start(out=out1_rows[:, t, :], in_=page[t][:])
+                if t < PACK - 1:
+                    for c in range(4):
+                        round_page(t, c)
+            if (t, h) == (0, 1):
+                w3_grouped = held("w3_grouped", [P, PACK * N], BF16, tag="grouped0")
+                for c0, c1 in ((0, 512), (512, N)):
+                    nc.scalar.copy(
+                        w3_grouped[:, PACK * c0 : PACK * c1].rearrange("p (c i t) -> p c t i", i=4, t=PACK),
+                        w3_raw[:, :, c0:c1].rearrange("p t (c i) -> p c t i", i=4),
+                    )
+                    nc.vector.quantize_mx(
+                        out=w3q[:, c0:c1].bitcast(FP8X4), scales=w3s[:, c0:c1],
+                        in_=w3_grouped[:, PACK * c0 : PACK * c1],
+                    )
+
+        out0_rows = out_0.rearrange("(b p) j -> p b j", p=P)
+        out2_words = out_2[0].rearrange("p m i -> p (m i)").bitcast(I32)
+        pq = [held(f"pq{i}", [P, 2 * BANK], U32) for i in range(2)]
+        ps = held("ps", [P, T2], U8)
+        for c in range(PJ // CHUNK):
+            picked = held(f"picked{c}", [P, PACK, CHUNK], F32, tag=f"ring{c % 2}")
+            xb = held(f"xb{c}", [P, PACK, CHUNK], BF16, tag="xb", bufs=2)
+            for t in range(PACK):
+                nc.vector.tensor_copy(
+                    picked[:, t, :], page[t][:].indirect(offs3_t[:, 16 * c : 16 * c + 16])
+                )
+                nc.scalar.activation(
+                    xb[:, t, :], picked[:, t, :], ACT.Identity, bias=bias_t[:, t : t + 1]
+                )
+            xil = held(f"xil{c}", [P, PACK * CHUNK], BF16, tag=f"ring{c % 2}")
+            nc.scalar.copy(
+                xil[:].rearrange("p (c i t) -> p c t i", i=4, t=PACK),
+                xb[:].rearrange("p t (c i) -> p c t i", i=4),
+            )
+            xq = held(f"xq{c}", [P, CHUNK], U32)
+            xs = held(f"xs{c}", [P, CHUNK], U8)
+            nc.vector.quantize_mx(out=xq[:].bitcast(FP8X4), scales=xs[:], in_=xil[:])
+            y = held(f"y{c}", [P, NT, CHUNK], F32, tag="w1_raw_y", bufs=2)
+            for k in range(NT // 2):
+                acc_e = bank(f"e{c}_{k}", [P, 2, CHUNK])
+                acc_f = bank(f"f{c}_{k}", [P, 2, CHUNK])
+                for acc, codes, scales in ((acc_e, w3q, w3s), (acc_f, w4, w4s)):
+                    for i in range(2):
+                        cols = slice((2 * k + i) * P, (2 * k + i + 1) * P)
+                        nc.tensor.matmul_mx(
+                            out=acc[:, i, :], lhsT=codes[:, cols].bitcast(FP8X4),
+                            lhsT_scale=scales[:, cols], rhs=xq[:].bitcast(FP8X4), rhs_scale=xs[:],
+                            start=True, stop=True,
+                        )
+                mag = held(f"mag{c}_{k}", [P, 2, CHUNK], F32, tag="evac", bufs=3)
+                nc.scalar.activation(mag[:], acc_e[:], ACT.Abs)
+                prod = held(f"prod{c}_{k}", [P, 2, CHUNK], F32, tag="m_prod", bufs=8)
+                nc.vector.tensor_tensor(prod[:], acc_f[:], mag[:], ALU.mult)
+                j0 = (c % 2) * CHUNK
+                nc.gpsimd.tensor_tensor(
+                    y[:, 2 * k : 2 * k + 2, :], prod[:],
+                    delay_t[c // 2][:, 2 * k : 2 * k + 2, j0 : j0 + CHUNK], ALU.add,
+                )
+            nc.sync.dma_start(out=out0_rows[:, :, c * CHUNK : (c + 1) * CHUNK], in_=y[:])
+
+            round_page(PACK - 1, c)
+            nc.vector.quantize_mx(
+                out=pq[c // 2][:, (c % 2) * BANK : (c % 2 + 1) * BANK].bitcast(FP8X4),
+                scales=ps[:, c * BANK : (c + 1) * BANK],
+                in_=pil[c][:].rearrange("p m t -> p (m t)"),
+            )
+            if c % 2 == 1:
+                nc.sync.dma_start(
+                    out=out2_words[:, (c - 1) * BANK : (c + 1) * BANK], in_=pq[c // 2][:].bitcast(I32)
+                )
+        for q in range(4):
+            nc.sync.dma_start(
+                out=out_3[0, 4 * q : 4 * q + 4, :].bitcast(I32),
+                in_=ps[32 * q : 32 * q + 4, :].bitcast(I32),
+            )

@@ -23,6 +23,11 @@ PASSES = K // (P * PACK)
 BANK = 512
 CHUNK = 256
 NT = N // P
+ORDER = "f0 f1 b0 f2 b1 f3 p0 p1 b2 b3"
+XBUFS = 2
+VIL = ()
+VADD = ((3, 2),)
+SPLIT = (3,)
 
 
 def tile_list_blast_hole_charging_kernel(
@@ -61,7 +66,7 @@ def tile_list_blast_hole_charging_kernel(
 
         offs_t = lists.tile([P, S // 16], U16, name="offs_t")
         nc.sync.dma_start(offs_t[:], offs)
-        wgs_t = held("wgs_t", [P, S], F32)
+        wgs_t = held("wgs_t", [P, S], F32, tag="wgs_tab0")
         nc.sync.dma_start(out=wgs_t[:], in_=wgs)
         gain_t = held("gain_t", [P, PACK], F32)
         nc.sync.dma_start(out=gain_t[:], in_=gain.rearrange("(p t) -> p t", t=PACK))
@@ -71,23 +76,27 @@ def tile_list_blast_hole_charging_kernel(
         )
         w1_raw = []
         for a in range(PASSES):
-            raw = held(f"w1_raw{a}", [P, PACK, H], F32, tag="w1_raw_y", bufs=2)
+            raw = held(f"w1_raw{a}", [P, PACK, H], F32, tag=f"w1_raw{a}")
             nc.sync.dma_start(
                 out=raw[:], in_=w1[a * 512 : (a + 1) * 512, :].rearrange("(p j) c -> p j c", j=PACK)
             )
             w1_raw.append(raw)
-        tab = []
-        for a in range(PASSES):
-            words = held(f"tab{a}", [P, T], I32, tag=f"tab_delay{a}")
-            nc.sync.dma_start(
-                out=words[:], in_=tab_words[a].rearrange("p t i -> p (t i)").bitcast(I32)
-            )
-            tab.append(words)
         offs2_t = lists.tile([P, S // 16], U16, name="offs2_t")
         nc.sync.dma_start(offs2_t[:], offs2)
         page_rows = page0.rearrange("(p t) m -> p t m", t=PACK)
-        page = [held(f"page{t}", [P, T2], F32) for t in range(PACK)]
-        nc.sync.dma_start(out=page[0][:], in_=page_rows[:, 0, :])
+        page = []
+
+        def load_page(t, tag):
+            page.append(held(f"page{t}", [P, T2], F32, tag=tag))
+            nc.sync.dma_start(out=page[t][:], in_=page_rows[:, t, :])
+
+        tab = []
+
+        def load_tab(a, tag):
+            tab.append(held(f"tab{a}", [P, T], I32, tag=tag))
+            nc.sync.dma_start(
+                out=tab[a][:], in_=tab_words[a].rearrange("p t i -> p (t i)").bitcast(I32)
+            )
 
         gs = held("gs", [P, S], U8)
         nc.vector.tensor_copy(gs[:], ts[:].indirect(offs_t[:]))
@@ -98,10 +107,12 @@ def tile_list_blast_hole_charging_kernel(
         )
         nc.vector.tensor_copy(staged[:, :S].bitcast(I32), gs[:].bitcast(I32))
         for q in range(4):
-            nc.gpsimd.dma_start(
+            nc.scalar.dma_start(
                 out=tp[32 * q : 32 * q + 4, :, :].bitcast(I32),
                 in_=staged[32 * q : 32 * q + 32 : 4, :].bitcast(I32),
             )
+
+        load_page(0, "gs")
 
         wT = held("wT", [P, S // P, PACK, P], F32, tag="wT_w3")
         for half in range(2):
@@ -113,6 +124,7 @@ def tile_list_blast_hole_charging_kernel(
                 dst = wT[:, 4 * half : 4 * half + 4, :, 32 * q : 32 * q + 32]
                 src = turned[:].rearrange("j b (p t) -> j b t p", t=PACK)
                 nc.scalar.copy(dst, src)
+        load_tab(0, "wgs_tab0")
         wg = [held(f"wg{h}", [P, PACK, BANK], F32, tag=f"ring{h}") for h in range(2)]
         for t in range(PACK):
             for h in range(2):
@@ -126,17 +138,12 @@ def tile_list_blast_hole_charging_kernel(
 
         w3_raw = held("w3_raw", [P, PACK, N], F32, tag="wT_w3")
         nc.sync.dma_start(out=w3_raw[:], in_=w3.rearrange("(p j) c -> p j c", j=PACK))
-        nc.sync.dma_start(out=page[1][:], in_=page_rows[:, 1, :])
-        w4 = held("w4", [P, N], I32)
-        nc.sync.dma_start(out=w4[:], in_=w4_words[0].rearrange("p n i -> p (n i)").bitcast(I32))
-        nc.sync.dma_start(out=page[2][:], in_=page_rows[:, 2, :])
-        nc.sync.dma_start(out=page[3][:], in_=page_rows[:, 3, :])
         offs3_t = lists.tile([P, PJ // 16], U16, name="offs3_t")
         nc.sync.dma_start(offs3_t[:], offs3)
         bias_t = held("bias_t", [P, PACK], F32)
-        nc.sync.dma_start(out=bias_t[:], in_=bias.rearrange("(p t) -> p t", t=PACK))
+        nc.gpsimd.dma_start(out=bias_t[:], in_=bias.rearrange("(p t) -> p t", t=PACK))
         for q in range(4):
-            nc.sync.dma_start(
+            nc.gpsimd.dma_start(
                 out=w4s[32 * q : 32 * q + 4, :].bitcast(I32),
                 in_=w4_scales[0, 4 * q : 4 * q + 4, :].bitcast(I32),
             )
@@ -159,6 +166,8 @@ def tile_list_blast_hole_charging_kernel(
             w1q.append(codes)
             w1s.append(scales)
 
+        load_tab(1, "w1_raw0")
+
         gw = {}
         for a in range(PASSES):
             for h in range(2):
@@ -167,18 +176,19 @@ def tile_list_blast_hole_charging_kernel(
                     gw[a, h][:], tab[a][:].bitcast(U32).indirect(offs_t[:, 32 * h : 32 * h + 32])
                 )
 
-        delay_rows = delay.rearrange("(b p) j -> p b j", p=P)
-        delay_t = []
-        for h in range(2):
-            rows = held(f"delay{h}", [P, NT, BANK], F32, tag=f"tab_delay{h}")
-            nc.sync.dma_start(out=rows[:], in_=delay_rows[:, :, h * BANK : (h + 1) * BANK])
-            delay_t.append(rows)
+        load_page(1, "wgs_tab0")
+        load_page(2, "staged")
+        load_page(3, "w1_raw0")
 
         out1_rows = out_1.rearrange("(p t) m -> p t m", t=PACK)
-        pil = [held(f"pil{c}", [P, BANK, PACK], BF16) for c in range(4)]
+        pil = []
 
         def round_page(t, c):
-            nc.scalar.copy(pil[c][:, :, t], page[t][:, c * BANK : (c + 1) * BANK])
+            src = page[t][:, c * BANK : (c + 1) * BANK]
+            if t == 2:
+                nc.scalar.copy(pil[c][:, :, 2:4], src.unsqueeze(2).to_broadcast([P, BANK, 2]))
+            else:
+                nc.scalar.copy(pil[c][:, :, t], src)
 
         w3q = held("w3q", [P, N], U32)
         w3s = held("w3s", [P, N], U8)
@@ -202,7 +212,7 @@ def tile_list_blast_hole_charging_kernel(
                     lhsT_scale=tp[:, a, S + t * P : S + (t + 1) * P],
                     **moving,
                 )
-            a_sb = held(f"a_sb{t}_{h}", [P, BANK], F32, tag="evac", bufs=3)
+            a_sb = held(f"a_sb{t}_{h}", [P, BANK], F32, tag="evac", bufs=8)
             nc.scalar.copy(a_sb[:], acc_a[:])
             largest[t, h] = held(f"m{t}_{h}", [P, BANK], F32, tag="m_prod", bufs=8)
             nc.vector.tensor_tensor(largest[t, h][:], acc_b[:], a_sb[:], ALU.max)
@@ -221,9 +231,6 @@ def tile_list_blast_hole_charging_kernel(
             put(t, h)
             if h == 1:
                 nc.sync.dma_start(out=out1_rows[:, t, :], in_=page[t][:])
-                if t < PACK - 1:
-                    for c in range(4):
-                        round_page(t, c)
             if (t, h) == (0, 1):
                 w3_grouped = held("w3_grouped", [P, PACK * N], BF16, tag="grouped0")
                 for c0, c1 in ((0, 512), (512, N)):
@@ -236,13 +243,36 @@ def tile_list_blast_hole_charging_kernel(
                         in_=w3_grouped[:, PACK * c0 : PACK * c1],
                     )
 
+        for c in range(4):
+            pil.append(held(f"pil{c}", [P, BANK, PACK], BF16, tag=f"gw{c // 2}_{c % 2}"))
+        for t in range(PACK - 1):
+            for c in range(4):
+                round_page(t, c)
+        w4 = held("w4", [P, N], I32, tag="wT_w3")
+        nc.sync.dma_start(out=w4[:], in_=w4_words[0].rearrange("p n i -> p (n i)").bitcast(I32))
+        delay_rows = delay.rearrange("(b p) j -> p b j", p=P)
+        delay_t = []
+        for h, tag in enumerate(("grouped0", "w2d")):
+            rows = held(f"delay{h}", [P, NT, BANK], F32, tag=tag)
+            nc.sync.dma_start(out=rows[:], in_=delay_rows[:, :, h * BANK : (h + 1) * BANK])
+            delay_t.append(rows)
+
         out0_rows = out_0.rearrange("(b p) j -> p b j", p=P)
         out2_words = out_2[0].rearrange("p m i -> p (m i)").bitcast(I32)
-        pq = [held(f"pq{i}", [P, 2 * BANK], U32) for i in range(2)]
+        for c in range(4):
+            for half in range(2):
+                m0 = half * CHUNK
+                nc.gpsimd.tensor_scalar(
+                    pil[c][:, m0 : m0 + CHUNK, PACK - 1],
+                    page[PACK - 1][:, c * BANK + m0 : c * BANK + m0 + CHUNK],
+                    1.0, 0.0, ALU.mult, ALU.add,
+                )
         ps = held("ps", [P, T2], U8)
-        for c in range(PJ // CHUNK):
+        xq, xs = {}, {}
+
+        def front(c):
             picked = held(f"picked{c}", [P, PACK, CHUNK], F32, tag=f"ring{c % 2}")
-            xb = held(f"xb{c}", [P, PACK, CHUNK], BF16, tag="xb", bufs=2)
+            xb = held(f"xb{c}", [P, PACK, CHUNK], BF16, tag="xb", bufs=XBUFS)
             for t in range(PACK):
                 nc.vector.tensor_copy(
                     picked[:, t, :], page[t][:].indirect(offs3_t[:, 16 * c : 16 * c + 16])
@@ -251,14 +281,37 @@ def tile_list_blast_hole_charging_kernel(
                     xb[:, t, :], picked[:, t, :], ACT.Identity, bias=bias_t[:, t : t + 1]
                 )
             xil = held(f"xil{c}", [P, PACK * CHUNK], BF16, tag=f"ring{c % 2}")
-            nc.scalar.copy(
-                xil[:].rearrange("p (c i t) -> p c t i", i=4, t=PACK),
-                xb[:].rearrange("p t (c i) -> p c t i", i=4),
+            dst = xil[:].rearrange("p (c i t) -> p c t i", i=4, t=PACK)
+            src = xb[:].rearrange("p t (c i) -> p c t i", i=4)
+            if c in VIL:
+                nc.vector.tensor_copy(dst, src)
+            else:
+                nc.scalar.copy(dst, src)
+            xq[c] = held(f"xq{c}", [P, CHUNK], U32)
+            xs[c] = held(f"xs{c}", [P, CHUNK], U8)
+            nc.vector.quantize_mx(out=xq[c][:].bitcast(FP8X4), scales=xs[c][:], in_=xil[:])
+
+        def planes(half):
+            pq = held(f"pq{half}", [P, 2 * BANK], U32, tag=f"ring{half}")
+            for i in range(2):
+                m = 2 * half + i
+                nc.vector.quantize_mx(
+                    out=pq[:, i * BANK : (i + 1) * BANK].bitcast(FP8X4),
+                    scales=ps[:, m * BANK : (m + 1) * BANK],
+                    in_=pil[m][:].rearrange("p m t -> p (m t)"),
+                )
+            nc.sync.dma_start(
+                out=out2_words[:, 2 * half * BANK : 2 * (half + 1) * BANK], in_=pq[:].bitcast(I32)
             )
-            xq = held(f"xq{c}", [P, CHUNK], U32)
-            xs = held(f"xs{c}", [P, CHUNK], U8)
-            nc.vector.quantize_mx(out=xq[:].bitcast(FP8X4), scales=xs[:], in_=xil[:])
-            y = held(f"y{c}", [P, NT, CHUNK], F32, tag="w1_raw_y", bufs=2)
+            if half == 1:
+                for q in range(4):
+                    nc.sync.dma_start(
+                        out=out_3[0, 4 * q : 4 * q + 4, :].bitcast(I32),
+                        in_=ps[32 * q : 32 * q + 4, :].bitcast(I32),
+                    )
+
+        def back(c):
+            y = held(f"y{c}", [P, NT, CHUNK], F32, tag="y", bufs=4)
             for k in range(NT // 2):
                 acc_e = bank(f"e{c}_{k}", [P, 2, CHUNK])
                 acc_f = bank(f"f{c}_{k}", [P, 2, CHUNK])
@@ -267,32 +320,25 @@ def tile_list_blast_hole_charging_kernel(
                         cols = slice((2 * k + i) * P, (2 * k + i + 1) * P)
                         nc.tensor.matmul_mx(
                             out=acc[:, i, :], lhsT=codes[:, cols].bitcast(FP8X4),
-                            lhsT_scale=scales[:, cols], rhs=xq[:].bitcast(FP8X4), rhs_scale=xs[:],
+                            lhsT_scale=scales[:, cols], rhs=xq[c][:].bitcast(FP8X4), rhs_scale=xs[c][:],
                             start=True, stop=True,
                         )
-                mag = held(f"mag{c}_{k}", [P, 2, CHUNK], F32, tag="evac", bufs=3)
+                mag = held(f"mag{c}_{k}", [P, 2, CHUNK], F32, tag="evac", bufs=8)
                 nc.scalar.activation(mag[:], acc_e[:], ACT.Abs)
                 prod = held(f"prod{c}_{k}", [P, 2, CHUNK], F32, tag="m_prod", bufs=8)
                 nc.vector.tensor_tensor(prod[:], acc_f[:], mag[:], ALU.mult)
                 j0 = (c % 2) * CHUNK
-                nc.gpsimd.tensor_tensor(
+                (nc.vector if (c, k) in VADD else nc.gpsimd).tensor_tensor(
                     y[:, 2 * k : 2 * k + 2, :], prod[:],
                     delay_t[c // 2][:, 2 * k : 2 * k + 2, j0 : j0 + CHUNK], ALU.add,
                 )
-            nc.sync.dma_start(out=out0_rows[:, :, c * CHUNK : (c + 1) * CHUNK], in_=y[:])
+                if c in SPLIT:
+                    nc.sync.dma_start(
+                        out=out0_rows[:, 2 * k : 2 * k + 2, c * CHUNK : (c + 1) * CHUNK],
+                        in_=y[:, 2 * k : 2 * k + 2, :],
+                    )
+            if c not in SPLIT:
+                nc.sync.dma_start(out=out0_rows[:, :, c * CHUNK : (c + 1) * CHUNK], in_=y[:])
 
-            round_page(PACK - 1, c)
-            nc.vector.quantize_mx(
-                out=pq[c // 2][:, (c % 2) * BANK : (c % 2 + 1) * BANK].bitcast(FP8X4),
-                scales=ps[:, c * BANK : (c + 1) * BANK],
-                in_=pil[c][:].rearrange("p m t -> p (m t)"),
-            )
-            if c % 2 == 1:
-                nc.sync.dma_start(
-                    out=out2_words[:, (c - 1) * BANK : (c + 1) * BANK], in_=pq[c // 2][:].bitcast(I32)
-                )
-        for q in range(4):
-            nc.sync.dma_start(
-                out=out_3[0, 4 * q : 4 * q + 4, :].bitcast(I32),
-                in_=ps[32 * q : 32 * q + 4, :].bitcast(I32),
-            )
+        for step in ORDER.split():
+            {"f": front, "b": back, "p": planes}[step[0]](int(step[1]))

@@ -23,10 +23,15 @@ PASSES = K // (P * PACK)
 BANK = 512
 CHUNK = 256
 NT = N // P
-ORDER = "f0 f1 b0 f2 b1 f3 p0 p1 b2 b3"
+WIDTHS = (512, 512)
+GADD = ()
+STORES = (2, 5, 8, 9, 10, 11)
+SPIL = ()
+GPIL = ()
+ORDER = "r0 r1 f0 f1 p0 b0 r2 r3 p1 b1"
 XBUFS = 2
-VIL = ()
-VADD = ((3, 2),)
+VIL = (1,)
+VADD = ()
 SPLIT = (3,)
 
 
@@ -102,8 +107,8 @@ def tile_list_blast_hole_charging_kernel(
         nc.vector.tensor_copy(gs[:], ts[:].indirect(offs_t[:]))
         staged = held("staged", [P, S + H], U8)
         nc.vector.tensor_copy(
-            staged[:, S:].rearrange("p (t m) -> p m t", t=PACK),
-            w2s_raw[:].rearrange("p (m t) -> p m t", t=PACK),
+            staged[:, S:].rearrange("p (t m) -> p t m", t=PACK),
+            w2s_raw[:].rearrange("p (m t) -> p t m", t=PACK),
         )
         nc.vector.tensor_copy(staged[:, :S].bitcast(I32), gs[:].bitcast(I32))
         for q in range(4):
@@ -125,14 +130,14 @@ def tile_list_blast_hole_charging_kernel(
                 src = turned[:].rearrange("j b (p t) -> j b t p", t=PACK)
                 nc.scalar.copy(dst, src)
         load_tab(0, "wgs_tab0")
-        wg = [held(f"wg{h}", [P, PACK, BANK], F32, tag=f"ring{h}") for h in range(2)]
+        wg = [held(f"wg{t}", [P, S], F32) for t in range(PACK)]
         for t in range(PACK):
             for h in range(2):
                 back = bank(f"wgs{t}_{h}", [P, 4, P])
                 for b in range(4):
                     nc.tensor.transpose(back[:, b, :], wT[:, 4 * h + b, t, :], ident[:])
                 nc.scalar.activation(
-                    wg[h][:, t, :], back[:].rearrange("p b j -> p (b j)"), ACT.Copy,
+                    wg[t][:, h * BANK : (h + 1) * BANK], back[:].rearrange("p b j -> p (b j)"), ACT.Copy,
                     scale=gain_t[:, t : t + 1],
                 )
 
@@ -152,13 +157,13 @@ def tile_list_blast_hole_charging_kernel(
         w1q, w1s = [], []
         for a in range(PASSES):
             nc.vector.tensor_copy(
-                w2d[:, a, :, :].rearrange("p t (m b) -> p m t b", b=2),
-                w2_raw[:, a, :].rearrange("p (m t b) -> p m t b", t=PACK, b=2),
+                w2d[:, a, :, :].rearrange("p t (m b) -> p t m b", b=2),
+                w2_raw[:, a, :].rearrange("p (m t b) -> p t m b", t=PACK, b=2),
             )
             grouped = held(f"w1_grouped{a}", [P, PACK * H], BF16, tag=f"grouped{a}")
             nc.vector.tensor_copy(
-                grouped[:].rearrange("p (t m j) -> p m j t", t=PACK, j=PACK),
-                w1_raw[a][:].rearrange("p j (m t) -> p m j t", t=PACK),
+                grouped[:].rearrange("p (t m j) -> p m t j", t=PACK, j=PACK),
+                w1_raw[a][:].rearrange("p j (m t) -> p m t j", t=PACK),
             )
             codes = held(f"w1q{a}", [P, H], U32)
             scales = held(f"w1s{a}", [P, H], U8)
@@ -185,14 +190,14 @@ def tile_list_blast_hole_charging_kernel(
 
         def round_page(t, c):
             src = page[t][:, c * BANK : (c + 1) * BANK]
-            if t == 2:
+            if t == 2 and c in GPIL:
                 nc.scalar.copy(pil[c][:, :, 2:4], src.unsqueeze(2).to_broadcast([P, BANK, 2]))
             else:
                 nc.scalar.copy(pil[c][:, :, t], src)
 
         w3q = held("w3q", [P, N], U32)
         w3s = held("w3s", [P, N], U8)
-        largest = {}
+        largest = [held(f"m{t}", [P, S], F32) for t in range(PACK)]
 
         def first_products(t, h):
             cols = slice(t * P, (t + 1) * P)
@@ -214,24 +219,25 @@ def tile_list_blast_hole_charging_kernel(
                 )
             a_sb = held(f"a_sb{t}_{h}", [P, BANK], F32, tag="evac", bufs=8)
             nc.scalar.copy(a_sb[:], acc_a[:])
-            largest[t, h] = held(f"m{t}_{h}", [P, BANK], F32, tag="m_prod", bufs=8)
-            nc.vector.tensor_tensor(largest[t, h][:], acc_b[:], a_sb[:], ALU.max)
+            nc.vector.tensor_tensor(largest[t][:, h * BANK : (h + 1) * BANK], acc_b[:], a_sb[:], ALU.max)
 
-        def put(t, h):
+        def put(t, j0, j1):
             nc.vector.tensor_tensor(
-                page[t][:].indirect(offs2_t[:, 32 * h : 32 * h + 32]),
-                largest[t, h][:], wg[h][:, t, :], ALU.mult,
+                page[t][:].indirect(offs2_t[:, j0 // 16 : j1 // 16]),
+                largest[t][:, j0:j1], wg[t][:, j0:j1], ALU.mult,
             )
 
-        units = [(t, h) for t in range(PACK) for h in range(2)]
-        first_products(*units[0])
-        for i, (t, h) in enumerate(units):
-            if i + 1 < len(units):
-                first_products(*units[i + 1])
-            put(t, h)
-            if h == 1:
-                nc.sync.dma_start(out=out1_rows[:, t, :], in_=page[t][:])
-            if (t, h) == (0, 1):
+        first_products(0, 0)
+        put(0, 0, BANK)
+        first_products(0, 1)
+        for t in range(PACK):
+            if t + 1 < PACK:
+                first_products(t + 1, 0)
+            put(t, BANK if t == 0 else 0, S)
+            if t + 1 < PACK:
+                first_products(t + 1, 1)
+            nc.sync.dma_start(out=out1_rows[:, t, :], in_=page[t][:])
+            if t == 0:
                 w3_grouped = held("w3_grouped", [P, PACK * N], BF16, tag="grouped0")
                 for c0, c1 in ((0, 512), (512, N)):
                     nc.scalar.copy(
@@ -259,7 +265,7 @@ def tile_list_blast_hole_charging_kernel(
 
         out0_rows = out_0.rearrange("(b p) j -> p b j", p=P)
         out2_words = out_2[0].rearrange("p m i -> p (m i)").bitcast(I32)
-        for c in range(4):
+        for c in GPIL:
             for half in range(2):
                 m0 = half * CHUNK
                 nc.gpsimd.tensor_scalar(
@@ -271,28 +277,29 @@ def tile_list_blast_hole_charging_kernel(
         xq, xs = {}, {}
 
         def front(c):
-            picked = held(f"picked{c}", [P, PACK, CHUNK], F32, tag=f"ring{c % 2}")
-            xb = held(f"xb{c}", [P, PACK, CHUNK], BF16, tag="xb", bufs=XBUFS)
+            width, j0 = WIDTHS[c], sum(WIDTHS[:c])
+            picked = held(f"picked{c}", [P, PACK, width], F32, tag=("wg3", "m3")[c])
+            xb = held(f"xb{c}", [P, PACK, width], BF16, tag="xb", bufs=XBUFS)
             for t in range(PACK):
                 nc.vector.tensor_copy(
-                    picked[:, t, :], page[t][:].indirect(offs3_t[:, 16 * c : 16 * c + 16])
+                    picked[:, t, :], page[t][:].indirect(offs3_t[:, j0 // 16 : (j0 + width) // 16])
                 )
                 nc.scalar.activation(
                     xb[:, t, :], picked[:, t, :], ACT.Identity, bias=bias_t[:, t : t + 1]
                 )
-            xil = held(f"xil{c}", [P, PACK * CHUNK], BF16, tag=f"ring{c % 2}")
+            xil = held(f"xil{c}", [P, PACK * width], BF16, tag=f"xil{c}")
             dst = xil[:].rearrange("p (c i t) -> p c t i", i=4, t=PACK)
             src = xb[:].rearrange("p t (c i) -> p c t i", i=4)
             if c in VIL:
                 nc.vector.tensor_copy(dst, src)
             else:
                 nc.scalar.copy(dst, src)
-            xq[c] = held(f"xq{c}", [P, CHUNK], U32)
-            xs[c] = held(f"xs{c}", [P, CHUNK], U8)
+            xq[c] = held(f"xq{c}", [P, width], U32)
+            xs[c] = held(f"xs{c}", [P, width], U8)
             nc.vector.quantize_mx(out=xq[c][:].bitcast(FP8X4), scales=xs[c][:], in_=xil[:])
 
         def planes(half):
-            pq = held(f"pq{half}", [P, 2 * BANK], U32, tag=f"ring{half}")
+            pq = held(f"pq{half}", [P, 2 * BANK], U32, tag=f"xil{half}")
             for i in range(2):
                 m = 2 * half + i
                 nc.vector.quantize_mx(
@@ -311,34 +318,34 @@ def tile_list_blast_hole_charging_kernel(
                     )
 
         def back(c):
-            y = held(f"y{c}", [P, NT, CHUNK], F32, tag="y", bufs=4)
-            for k in range(NT // 2):
-                acc_e = bank(f"e{c}_{k}", [P, 2, CHUNK])
-                acc_f = bank(f"f{c}_{k}", [P, 2, CHUNK])
+            width, j0 = WIDTHS[c], sum(WIDTHS[:c])
+            per = BANK // width
+            y = held(f"y{c}", [P, NT, width], F32, tag=("w1_raw1", "ts")[c])
+            for k in range(NT // per):
+                rows = slice(per * k, per * (k + 1))
+                acc_e = bank(f"e{c}_{k}", [P, per, width])
+                acc_f = bank(f"f{c}_{k}", [P, per, width])
                 for acc, codes, scales in ((acc_e, w3q, w3s), (acc_f, w4, w4s)):
-                    for i in range(2):
-                        cols = slice((2 * k + i) * P, (2 * k + i + 1) * P)
+                    for i in range(per):
+                        cols = slice((per * k + i) * P, (per * k + i + 1) * P)
                         nc.tensor.matmul_mx(
                             out=acc[:, i, :], lhsT=codes[:, cols].bitcast(FP8X4),
                             lhsT_scale=scales[:, cols], rhs=xq[c][:].bitcast(FP8X4), rhs_scale=xs[c][:],
                             start=True, stop=True,
                         )
-                mag = held(f"mag{c}_{k}", [P, 2, CHUNK], F32, tag="evac", bufs=8)
+                mag = held(f"mag{c}_{k}", [P, per, width], F32, tag="evac", bufs=8)
                 nc.scalar.activation(mag[:], acc_e[:], ACT.Abs)
-                prod = held(f"prod{c}_{k}", [P, 2, CHUNK], F32, tag="m_prod", bufs=8)
+                prod = held(f"prod{c}_{k}", [P, per, width], F32, tag=("m1", "m2", "wg0", "wg1", "wg2", "m0")[k % 6])
                 nc.vector.tensor_tensor(prod[:], acc_f[:], mag[:], ALU.mult)
-                j0 = (c % 2) * CHUNK
-                (nc.vector if (c, k) in VADD else nc.gpsimd).tensor_tensor(
-                    y[:, 2 * k : 2 * k + 2, :], prod[:],
-                    delay_t[c // 2][:, 2 * k : 2 * k + 2, j0 : j0 + CHUNK], ALU.add,
+                unit = j0 * NT // BANK + k
+                (nc.gpsimd if unit in GADD else nc.vector).tensor_tensor(
+                    y[:, rows, :], prod[:],
+                    delay_t[j0 // BANK][:, rows, j0 % BANK : j0 % BANK + width], ALU.add,
                 )
-                if c in SPLIT:
-                    nc.sync.dma_start(
-                        out=out0_rows[:, 2 * k : 2 * k + 2, c * CHUNK : (c + 1) * CHUNK],
-                        in_=y[:, 2 * k : 2 * k + 2, :],
-                    )
-            if c not in SPLIT:
-                nc.sync.dma_start(out=out0_rows[:, :, c * CHUNK : (c + 1) * CHUNK], in_=y[:])
+                if unit in STORES:
+                    first = max([u + 1 for u in STORES if u < unit] + [j0 * NT // BANK]) - j0 * NT // BANK
+                    done = slice(per * first, per * (k + 1))
+                    nc.sync.dma_start(out=out0_rows[:, done, j0 : j0 + width], in_=y[:, done, :])
 
         for step in ORDER.split():
-            {"f": front, "b": back, "p": planes}[step[0]](int(step[1]))
+            {"f": front, "b": back, "p": planes, "r": lambda c: round_page(PACK - 1, c)}[step[0]](int(step[1]))

@@ -19,20 +19,16 @@ ACT = mybir.ActivationFunctionType
 
 P = 128
 PACK = 4
-PASSES = K // (P * PACK)
+K_PASS = P * PACK
+PASSES = K // K_PASS
+QUADS = 4
+PER_COLUMN = 16
 BANK = 512
-CHUNK = 256
-NT = N // P
-WIDTHS = (512, 512)
-GADD = ()
-STORES = (2, 5, 8, 9, 10, 11)
-SPIL = ()
-GPIL = ()
-ORDER = "r0 r1 f0 f1 p0 b0 r2 r3 p1 b1"
-XBUFS = 2
-VIL = (1,)
-VADD = ()
-SPLIT = (3,)
+HALVES = 2
+N_TILES = N // P
+QUARTERS = T2 // BANK
+BANKS = {"scalar": 3, "vector": 5}
+STAGED = HALVES * PACK - 1
 
 
 def tile_list_blast_hole_charging_kernel(
@@ -43,35 +39,50 @@ def tile_list_blast_hole_charging_kernel(
     with ExitStack() as ctx:
         lists = ctx.enter_context(tc.tile_pool(name="lists", bufs=1))
         keep = ctx.enter_context(tc.tile_pool(name="keep", bufs=1))
-        psum = ctx.enter_context(tc.psum_pool(name="psum", bufs=8))
+        psum = ctx.enter_context(tc.psum_pool(name="psum", bufs=1))
 
         def held(name, shape, dtype, tag=None, bufs=1):
             return keep.tile(shape, dtype, name=name, tag=tag or name, bufs=bufs, align_bytes=64)
 
-        def bank(name, shape):
-            return psum.tile(shape, F32, name=name, tag="bank")
+        def bank(name, shape, reader):
+            return psum.tile(shape, F32, name=name, tag=reader, bufs=BANKS[reader])
 
-        ts = held("ts", [P, T], U8)
-        nc.vector.memset(ts[:].bitcast(I32), 0)
-        w2s_raw = held("w2s_raw", [P, H], U8)
-        nc.vector.memset(w2s_raw[:].bitcast(I32), 0)
-        tp = held("tp", [P, PASSES, S + H], U8)
-        nc.vector.memset(tp[:].rearrange("p a c -> p (a c)").bitcast(I32), 0)
-        w4s = held("w4s", [P, N], U8)
-        nc.vector.memset(w4s[:].bitcast(I32), 0)
+        def half_cols(h):
+            return slice(h * BANK, (h + 1) * BANK)
 
-        nc.gpsimd.dma_start(
-            out=ts[0:P:4, :].bitcast(I32), in_=tab_scales.rearrange("a q t -> q a t").bitcast(I32)
+        def entries(list_tile, j0, j1):
+            return list_tile[:, j0 // PER_COLUMN : j1 // PER_COLUMN]
+
+        def live_rows(q):
+            return slice(32 * q, 32 * q + 4)
+
+        def interleave(copy, dst, src):
+            copy(
+                dst.rearrange("p (c i t) -> p c t i", i=4, t=PACK),
+                src.rearrange("p t (c i) -> p c t i", i=4),
+            )
+
+        tab_rows = held("tab_rows", [P, T], U8)
+        nc.vector.memset(tab_rows[:].bitcast(I32), 0)
+        w2_rows = held("w2_rows", [P, H], U8)
+        nc.vector.memset(w2_rows[:].bitcast(I32), 0)
+        planes = held("planes", [P, PASSES, S + H], U8)
+        nc.vector.memset(planes[:].rearrange("p a c -> p (a c)").bitcast(I32), 0)
+        w4_plane = held("w4_plane", [P, N], U8)
+        nc.vector.memset(w4_plane[:].bitcast(I32), 0)
+
+        nc.sync.dma_start(
+            out=tab_rows[0:P:4, :].bitcast(I32), in_=tab_scales.rearrange("a q t -> q a t").bitcast(I32)
         )
-        nc.gpsimd.dma_start(
-            out=w2s_raw[0:P:4, :].bitcast(I32), in_=w2_scales.rearrange("a q c -> q a c").bitcast(I32)
+        nc.sync.dma_start(
+            out=w2_rows[0:P:4, :].bitcast(I32), in_=w2_scales.rearrange("a q c -> q a c").bitcast(I32)
         )
         ident = held("ident", [P, P], F32)
         make_identity(nc, ident[:])
 
-        offs_t = lists.tile([P, S // 16], U16, name="offs_t")
+        offs_t = lists.tile([P, S // PER_COLUMN], U16, name="offs_t")
         nc.sync.dma_start(offs_t[:], offs)
-        wgs_t = held("wgs_t", [P, S], F32, tag="wgs_tab0")
+        wgs_t = held("wgs_t", [P, S], F32)
         nc.sync.dma_start(out=wgs_t[:], in_=wgs)
         gain_t = held("gain_t", [P, PACK], F32)
         nc.sync.dma_start(out=gain_t[:], in_=gain.rearrange("(p t) -> p t", t=PACK))
@@ -81,13 +92,14 @@ def tile_list_blast_hole_charging_kernel(
         )
         w1_raw = []
         for a in range(PASSES):
-            raw = held(f"w1_raw{a}", [P, PACK, H], F32, tag=f"w1_raw{a}")
+            w1_raw.append(held(f"w1_raw{a}", [P, PACK, H], F32))
             nc.sync.dma_start(
-                out=raw[:], in_=w1[a * 512 : (a + 1) * 512, :].rearrange("(p j) c -> p j c", j=PACK)
+                out=w1_raw[a][:],
+                in_=w1[a * K_PASS : (a + 1) * K_PASS, :].rearrange("(p j) c -> p j c", j=PACK),
             )
-            w1_raw.append(raw)
-        offs2_t = lists.tile([P, S // 16], U16, name="offs2_t")
+        offs2_t = lists.tile([P, S // PER_COLUMN], U16, name="offs2_t")
         nc.sync.dma_start(offs2_t[:], offs2)
+
         page_rows = page0.rearrange("(p t) m -> p t m", t=PACK)
         page = []
 
@@ -103,249 +115,242 @@ def tile_list_blast_hole_charging_kernel(
                 out=tab[a][:], in_=tab_words[a].rearrange("p t i -> p (t i)").bitcast(I32)
             )
 
-        gs = held("gs", [P, S], U8)
-        nc.vector.tensor_copy(gs[:], ts[:].indirect(offs_t[:]))
-        staged = held("staged", [P, S + H], U8)
-        nc.vector.tensor_copy(
-            staged[:, S:].rearrange("p (t m) -> p t m", t=PACK),
-            w2s_raw[:].rearrange("p (m t) -> p t m", t=PACK),
-        )
-        nc.vector.tensor_copy(staged[:, :S].bitcast(I32), gs[:].bitcast(I32))
-        for q in range(4):
-            nc.scalar.dma_start(
-                out=tp[32 * q : 32 * q + 4, :, :].bitcast(I32),
-                in_=staged[32 * q : 32 * q + 32 : 4, :].bitcast(I32),
-            )
+        wgs_turned = held("wgs_turned", [P, S // P, PACK, P], F32)
+        blocks = BANK // P
+        for h in range(HALVES):
+            turned = bank(f"turned{h}", [P, blocks, P], "scalar")
+            for b in range(blocks):
+                j0 = h * BANK + b * P
+                nc.tensor.transpose(turned[:, b, :], wgs_t[:, j0 : j0 + P], ident[:])
+            for q in range(QUADS):
+                nc.scalar.copy(
+                    wgs_turned[:, blocks * h : blocks * (h + 1), :, 32 * q : 32 * (q + 1)],
+                    turned[:].rearrange("j b (p t) -> j b t p", t=PACK),
+                )
+        load_tab(0, "wgs_t")
+        pieces = [(0, 0, BANK), (0, BANK, S)] + [(t, 0, S) for t in range(1, PACK)]
+        weight = [held(f"weight{i}", [P, j1 - j0], F32) for i, (t, j0, j1) in enumerate(pieces)]
 
-        load_page(0, "gs")
+        def in_piece(tiles, t, h):
+            return tiles[h][:] if t == 0 else tiles[t + 1][:, half_cols(h)]
 
-        wT = held("wT", [P, S // P, PACK, P], F32, tag="wT_w3")
-        for half in range(2):
-            turned = bank(f"wgsT{half}", [P, 4, P])
-            for b in range(4):
-                jb = 4 * half + b
-                nc.tensor.transpose(turned[:, b, :], wgs_t[:, jb * P : (jb + 1) * P], ident[:])
-            for q in range(4):
-                dst = wT[:, 4 * half : 4 * half + 4, :, 32 * q : 32 * q + 32]
-                src = turned[:].rearrange("j b (p t) -> j b t p", t=PACK)
-                nc.scalar.copy(dst, src)
-        load_tab(0, "wgs_tab0")
-        wg = [held(f"wg{t}", [P, S], F32) for t in range(PACK)]
-        for t in range(PACK):
-            for h in range(2):
-                back = bank(f"wgs{t}_{h}", [P, 4, P])
-                for b in range(4):
-                    nc.tensor.transpose(back[:, b, :], wT[:, 4 * h + b, t, :], ident[:])
+        def make_weight(t):
+            for h in range(HALVES):
+                back = bank(f"back{t}_{h}", [P, blocks, P], "vector")
+                for b in range(blocks):
+                    nc.tensor.transpose(back[:, b, :], wgs_turned[:, blocks * h + b, t, :], ident[:])
                 nc.scalar.activation(
-                    wg[t][:, h * BANK : (h + 1) * BANK], back[:].rearrange("p b j -> p (b j)"), ACT.Copy,
+                    in_piece(weight, t, h), back[:].rearrange("p b j -> p (b j)"), ACT.Copy,
                     scale=gain_t[:, t : t + 1],
                 )
 
-        w3_raw = held("w3_raw", [P, PACK, N], F32, tag="wT_w3")
-        nc.sync.dma_start(out=w3_raw[:], in_=w3.rearrange("(p j) c -> p j c", j=PACK))
-        offs3_t = lists.tile([P, PJ // 16], U16, name="offs3_t")
+        make_weight(0)
+
+        offs3_t = lists.tile([P, PJ // PER_COLUMN], U16, name="offs3_t")
         nc.sync.dma_start(offs3_t[:], offs3)
         bias_t = held("bias_t", [P, PACK], F32)
         nc.gpsimd.dma_start(out=bias_t[:], in_=bias.rearrange("(p t) -> p t", t=PACK))
-        for q in range(4):
+        for q in range(QUADS):
             nc.gpsimd.dma_start(
-                out=w4s[32 * q : 32 * q + 4, :].bitcast(I32),
+                out=w4_plane[live_rows(q), :].bitcast(I32),
                 in_=w4_scales[0, 4 * q : 4 * q + 4, :].bitcast(I32),
             )
 
-        w2d = held("w2d", [P, PASSES, PACK, 2 * P], U8)
-        w1q, w1s = [], []
+        w2_codes = held("w2_codes", [P, PASSES, PACK, 2 * P], U8)
+        w1_codes, w1_plane = [], []
         for a in range(PASSES):
             nc.vector.tensor_copy(
-                w2d[:, a, :, :].rearrange("p t (m b) -> p t m b", b=2),
+                w2_codes[:, a, :, :].rearrange("p t (m b) -> p t m b", b=2),
                 w2_raw[:, a, :].rearrange("p (m t b) -> p t m b", t=PACK, b=2),
             )
-            grouped = held(f"w1_grouped{a}", [P, PACK * H], BF16, tag=f"grouped{a}")
+            grouped = held(f"w1_grouped{a}", [P, PACK * H], BF16)
             nc.vector.tensor_copy(
                 grouped[:].rearrange("p (t m j) -> p m t j", t=PACK, j=PACK),
                 w1_raw[a][:].rearrange("p j (m t) -> p m t j", t=PACK),
             )
-            codes = held(f"w1q{a}", [P, H], U32)
-            scales = held(f"w1s{a}", [P, H], U8)
-            nc.vector.quantize_mx(out=codes[:].bitcast(FP8X4), scales=scales[:], in_=grouped[:])
-            w1q.append(codes)
-            w1s.append(scales)
+            w1_codes.append(held(f"w1_codes{a}", [P, H], U32))
+            w1_plane.append(held(f"w1_plane{a}", [P, H], U8))
+            nc.vector.quantize_mx(out=w1_codes[a][:].bitcast(FP8X4), scales=w1_plane[a][:], in_=grouped[:])
 
-        load_tab(1, "w1_raw0")
+        load_tab(1, "w2_raw")
 
-        gw = {}
+        picked_scales = held("picked_scales", [P, S], U8, tag="w1_raw1")
+        nc.vector.tensor_copy(picked_scales[:], tab_rows[:].indirect(offs_t[:]))
+        scale_rows = held("scale_rows", [P, S + H], U8, tag="w1_grouped0")
+        nc.vector.tensor_copy(
+            scale_rows[:, S:].rearrange("p (t m) -> p t m", t=PACK),
+            w2_rows[:].rearrange("p (m t) -> p t m", t=PACK),
+        )
+        nc.vector.tensor_copy(scale_rows[:, :S].bitcast(I32), picked_scales[:].bitcast(I32))
+        for q in range(QUADS):
+            nc.sync.dma_start(
+                out=planes[live_rows(q), :, :].bitcast(I32),
+                in_=scale_rows[32 * q : 32 * (q + 1) : 4, :].bitcast(I32),
+            )
+
+        load_page(0, "w1_raw1")
+        for t in range(1, PACK):
+            make_weight(t)
+
+        v_codes = {}
         for a in range(PASSES):
-            for h in range(2):
-                gw[a, h] = held(f"gw{a}_{h}", [P, BANK], U32)
+            for h in range(HALVES):
+                v_codes[a, h] = held(f"v_codes{a}_{h}", [P, BANK], U32)
                 nc.vector.tensor_copy(
-                    gw[a, h][:], tab[a][:].bitcast(U32).indirect(offs_t[:, 32 * h : 32 * h + 32])
+                    v_codes[a, h][:],
+                    tab[a][:].bitcast(U32).indirect(entries(offs_t, h * BANK, (h + 1) * BANK)),
                 )
 
-        load_page(1, "wgs_tab0")
-        load_page(2, "staged")
-        load_page(3, "w1_raw0")
+        w3_raw = held("w3_raw", [P, PACK, N], F32, tag="wgs_t")
+        nc.sync.dma_start(out=w3_raw[:], in_=w3.rearrange("(p j) c -> p j c", j=PACK))
+        load_page(1, "w2_raw")
 
-        out1_rows = out_1.rearrange("(p t) m -> p t m", t=PACK)
-        pil = []
-
-        def round_page(t, c):
-            src = page[t][:, c * BANK : (c + 1) * BANK]
-            if t == 2 and c in GPIL:
-                nc.scalar.copy(pil[c][:, :, 2:4], src.unsqueeze(2).to_broadcast([P, BANK, 2]))
-            else:
-                nc.scalar.copy(pil[c][:, :, t], src)
-
-        w3q = held("w3q", [P, N], U32)
-        w3s = held("w3s", [P, N], U8)
-        largest = [held(f"m{t}", [P, S], F32) for t in range(PACK)]
+        largest = []
 
         def first_products(t, h):
             cols = slice(t * P, (t + 1) * P)
-            acc_a = bank(f"a{t}_{h}", [P, BANK])
-            acc_b = bank(f"b{t}_{h}", [P, BANK])
+            acc_a = bank(f"a{t}_{h}", [P, BANK], "scalar")
+            acc_b = bank(f"b{t}_{h}", [P, BANK], "vector")
             for a in range(PASSES):
                 moving = dict(
-                    rhs=gw[a, h][:].bitcast(FP8X4), rhs_scale=tp[:, a, h * BANK : (h + 1) * BANK],
+                    rhs=v_codes[a, h][:].bitcast(FP8X4), rhs_scale=planes[:, a, half_cols(h)],
                     start=(a == 0), stop=(a == PASSES - 1),
                 )
                 nc.tensor.matmul_mx(
-                    out=acc_a[:], lhsT=w1q[a][:, cols].bitcast(FP8X4), lhsT_scale=w1s[a][:, cols],
-                    **moving,
+                    out=acc_a[:], lhsT=w1_codes[a][:, cols].bitcast(FP8X4),
+                    lhsT_scale=w1_plane[a][:, cols], **moving,
                 )
                 nc.tensor.matmul_mx(
-                    out=acc_b[:], lhsT=w2d[:, a, t, :].bitcast(FP4X4),
-                    lhsT_scale=tp[:, a, S + t * P : S + (t + 1) * P],
-                    **moving,
+                    out=acc_b[:], lhsT=w2_codes[:, a, t, :].bitcast(FP4X4),
+                    lhsT_scale=planes[:, a, S + t * P : S + (t + 1) * P], **moving,
                 )
-            a_sb = held(f"a_sb{t}_{h}", [P, BANK], F32, tag="evac", bufs=8)
+            if (t, h) == (0, 1):
+                a_sb = held("a_sb0_1", [P, BANK], F32)
+            else:
+                a_sb = held(f"a_sb{t}_{h}", [P, BANK], F32, tag="staged", bufs=STAGED)
             nc.scalar.copy(a_sb[:], acc_a[:])
-            nc.vector.tensor_tensor(largest[t][:, h * BANK : (h + 1) * BANK], acc_b[:], a_sb[:], ALU.max)
+            nc.vector.tensor_tensor(in_piece(largest, t, h), acc_b[:], a_sb[:], ALU.max)
 
-        def put(t, j0, j1):
+        def put(i):
+            t, j0, j1 = pieces[i]
             nc.vector.tensor_tensor(
-                page[t][:].indirect(offs2_t[:, j0 // 16 : j1 // 16]),
-                largest[t][:, j0:j1], wg[t][:, j0:j1], ALU.mult,
+                page[t][:].indirect(entries(offs2_t, j0, j1)), largest[i][:], weight[i][:], ALU.mult
             )
 
-        first_products(0, 0)
-        put(0, 0, BANK)
-        first_products(0, 1)
-        for t in range(PACK):
-            if t + 1 < PACK:
-                first_products(t + 1, 0)
-            put(t, BANK if t == 0 else 0, S)
-            if t + 1 < PACK:
-                first_products(t + 1, 1)
-            nc.sync.dma_start(out=out1_rows[:, t, :], in_=page[t][:])
-            if t == 0:
-                w3_grouped = held("w3_grouped", [P, PACK * N], BF16, tag="grouped0")
-                for c0, c1 in ((0, 512), (512, N)):
-                    nc.scalar.copy(
-                        w3_grouped[:, PACK * c0 : PACK * c1].rearrange("p (c i t) -> p c t i", i=4, t=PACK),
-                        w3_raw[:, :, c0:c1].rearrange("p t (c i) -> p c t i", i=4),
-                    )
-                    nc.vector.quantize_mx(
-                        out=w3q[:, c0:c1].bitcast(FP8X4), scales=w3s[:, c0:c1],
-                        in_=w3_grouped[:, PACK * c0 : PACK * c1],
-                    )
+        w3_codes = held("w3_codes", [P, N], U32)
+        w3_plane = held("w3_plane", [P, N], U8)
 
-        for c in range(4):
-            pil.append(held(f"pil{c}", [P, BANK, PACK], BF16, tag=f"gw{c // 2}_{c % 2}"))
+        def quantise_w3():
+            w3_grouped = held("w3_grouped", [P, PACK * N], BF16, tag="a_sb0_1")
+            for c0, c1 in ((0, BANK), (BANK, N)):
+                interleave(nc.scalar.copy, w3_grouped[:, PACK * c0 : PACK * c1], w3_raw[:, :, c0:c1])
+                nc.vector.quantize_mx(
+                    out=w3_codes[:, c0:c1].bitcast(FP8X4), scales=w3_plane[:, c0:c1],
+                    in_=w3_grouped[:, PACK * c0 : PACK * c1],
+                )
+
+        out1_rows = out_1.rearrange("(p t) m -> p t m", t=PACK)
+        largest_tags = ("largest0", "largest0", "weight0", "weight1", "largest4")
+        page_tags = {1: "largest0", 2: "weight0"}
+        for i, (t, j0, j1) in enumerate(pieces):
+            largest.append(held(f"largest{i}", [P, j1 - j0], F32, tag=largest_tags[i]))
+            for h in range(j0 // BANK, j1 // BANK):
+                first_products(t, h)
+            put(i)
+            if j1 == S:
+                nc.sync.dma_start(out=out1_rows[:, t, :], in_=page[t][:])
+            if i in page_tags:
+                load_page(i + 1, page_tags[i])
+            if i == 2:
+                quantise_w3()
+
+        page_grouped = [
+            held(f"page_grouped{c}", [P, BANK, PACK], BF16, tag=f"v_codes{c // HALVES}_{c % HALVES}")
+            for c in range(QUARTERS)
+        ]
+
+        def round_page(t, c):
+            nc.scalar.copy(page_grouped[c][:, :, t], page[t][:, c * BANK : (c + 1) * BANK])
+
         for t in range(PACK - 1):
-            for c in range(4):
+            for c in range(QUARTERS):
                 round_page(t, c)
-        w4 = held("w4", [P, N], I32, tag="wT_w3")
-        nc.sync.dma_start(out=w4[:], in_=w4_words[0].rearrange("p n i -> p (n i)").bitcast(I32))
+
+        w4_codes = held("w4_codes", [P, N], I32, tag="wgs_t")
+        nc.sync.dma_start(out=w4_codes[:], in_=w4_words[0].rearrange("p n i -> p (n i)").bitcast(I32))
         delay_rows = delay.rearrange("(b p) j -> p b j", p=P)
         delay_t = []
-        for h, tag in enumerate(("grouped0", "w2d")):
-            rows = held(f"delay{h}", [P, NT, BANK], F32, tag=tag)
-            nc.sync.dma_start(out=rows[:], in_=delay_rows[:, :, h * BANK : (h + 1) * BANK])
-            delay_t.append(rows)
+        for h, tag in enumerate(("a_sb0_1", "w2_codes")):
+            delay_t.append(held(f"delay{h}", [P, N_TILES, BANK], F32, tag=tag))
+            nc.sync.dma_start(out=delay_t[h][:], in_=delay_rows[:, :, half_cols(h)])
 
         out0_rows = out_0.rearrange("(b p) j -> p b j", p=P)
         out2_words = out_2[0].rearrange("p m i -> p (m i)").bitcast(I32)
-        for c in GPIL:
-            for half in range(2):
-                m0 = half * CHUNK
-                nc.gpsimd.tensor_scalar(
-                    pil[c][:, m0 : m0 + CHUNK, PACK - 1],
-                    page[PACK - 1][:, c * BANK + m0 : c * BANK + m0 + CHUNK],
-                    1.0, 0.0, ALU.mult, ALU.add,
-                )
-        ps = held("ps", [P, T2], U8)
-        xq, xs = {}, {}
+        page_plane = held("page_plane", [P, T2], U8)
+        x_codes, x_plane = [], []
 
-        def front(c):
-            width, j0 = WIDTHS[c], sum(WIDTHS[:c])
-            picked = held(f"picked{c}", [P, PACK, width], F32, tag=("wg3", "m3")[c])
-            xb = held(f"xb{c}", [P, PACK, width], BF16, tag="xb", bufs=XBUFS)
+        def make_x(h):
+            picked = held(f"picked{h}", [P, PACK, BANK], F32, tag=("weight4", "largest4")[h])
+            rounded = held(f"rounded{h}", [P, PACK, BANK], BF16)
             for t in range(PACK):
                 nc.vector.tensor_copy(
-                    picked[:, t, :], page[t][:].indirect(offs3_t[:, j0 // 16 : (j0 + width) // 16])
+                    picked[:, t, :], page[t][:].indirect(entries(offs3_t, h * BANK, (h + 1) * BANK))
                 )
                 nc.scalar.activation(
-                    xb[:, t, :], picked[:, t, :], ACT.Identity, bias=bias_t[:, t : t + 1]
+                    rounded[:, t, :], picked[:, t, :], ACT.Identity, bias=bias_t[:, t : t + 1]
                 )
-            xil = held(f"xil{c}", [P, PACK * width], BF16, tag=f"xil{c}")
-            dst = xil[:].rearrange("p (c i t) -> p c t i", i=4, t=PACK)
-            src = xb[:].rearrange("p t (c i) -> p c t i", i=4)
-            if c in VIL:
-                nc.vector.tensor_copy(dst, src)
-            else:
-                nc.scalar.copy(dst, src)
-            xq[c] = held(f"xq{c}", [P, width], U32)
-            xs[c] = held(f"xs{c}", [P, width], U8)
-            nc.vector.quantize_mx(out=xq[c][:].bitcast(FP8X4), scales=xs[c][:], in_=xil[:])
+            x_grouped = held(f"x_grouped{h}", [P, PACK * BANK], BF16)
+            interleave((nc.scalar.copy, nc.vector.tensor_copy)[h], x_grouped[:], rounded[:])
+            x_codes.append(held(f"x_codes{h}", [P, BANK], U32))
+            x_plane.append(held(f"x_plane{h}", [P, BANK], U8))
+            nc.vector.quantize_mx(out=x_codes[h][:].bitcast(FP8X4), scales=x_plane[h][:], in_=x_grouped[:])
 
-        def planes(half):
-            pq = held(f"pq{half}", [P, 2 * BANK], U32, tag=f"xil{half}")
-            for i in range(2):
-                m = 2 * half + i
+        def quantise_page(h):
+            page_codes = held(f"page_codes{h}", [P, HALVES * BANK], U32, tag=f"x_grouped{h}")
+            for i in range(HALVES):
+                c = HALVES * h + i
                 nc.vector.quantize_mx(
-                    out=pq[:, i * BANK : (i + 1) * BANK].bitcast(FP8X4),
-                    scales=ps[:, m * BANK : (m + 1) * BANK],
-                    in_=pil[m][:].rearrange("p m t -> p (m t)"),
+                    out=page_codes[:, half_cols(i)].bitcast(FP8X4),
+                    scales=page_plane[:, c * BANK : (c + 1) * BANK],
+                    in_=page_grouped[c][:].rearrange("p m t -> p (m t)"),
                 )
             nc.sync.dma_start(
-                out=out2_words[:, 2 * half * BANK : 2 * (half + 1) * BANK], in_=pq[:].bitcast(I32)
+                out=out2_words[:, HALVES * h * BANK : HALVES * (h + 1) * BANK], in_=page_codes[:].bitcast(I32)
             )
-            if half == 1:
-                for q in range(4):
-                    nc.sync.dma_start(
-                        out=out_3[0, 4 * q : 4 * q + 4, :].bitcast(I32),
-                        in_=ps[32 * q : 32 * q + 4, :].bitcast(I32),
+
+        product_tags = ("weight1", "weight2", "weight3", "tab_rows", "w1_raw0", "w1_grouped1")
+
+        def second_products(h):
+            y = held(f"y{h}", [P, N_TILES, BANK], F32, tag=("wgs_turned", "w1_grouped0")[h])
+            for k in range(N_TILES):
+                cols = slice(k * P, (k + 1) * P)
+                acc_e = bank(f"e{h}_{k}", [P, BANK], "scalar")
+                acc_f = bank(f"f{h}_{k}", [P, BANK], "vector")
+                for acc, codes, plane in ((acc_e, w3_codes, w3_plane), (acc_f, w4_codes, w4_plane)):
+                    nc.tensor.matmul_mx(
+                        out=acc[:], lhsT=codes[:, cols].bitcast(FP8X4), lhsT_scale=plane[:, cols],
+                        rhs=x_codes[h][:].bitcast(FP8X4), rhs_scale=x_plane[h][:], start=True, stop=True,
                     )
+                size = held(f"size{h}_{k}", [P, BANK], F32, tag="staged", bufs=STAGED)
+                nc.scalar.activation(size[:], acc_e[:], ACT.Abs)
+                product = held(f"product{h}_{k}", [P, BANK], F32, tag=product_tags[k])
+                nc.vector.tensor_tensor(product[:], acc_f[:], size[:], ALU.mult)
+                last = h == HALVES - 1 and k == N_TILES - 1
+                adder = nc.gpsimd if k % 2 == 1 and not last else nc.vector
+                adder.tensor_tensor(y[:, k, :], product[:], delay_t[h][:, k, :], ALU.add)
+                nc.sync.dma_start(out=out0_rows[:, k, half_cols(h)], in_=y[:, k, :])
 
-        def back(c):
-            width, j0 = WIDTHS[c], sum(WIDTHS[:c])
-            per = BANK // width
-            y = held(f"y{c}", [P, NT, width], F32, tag=("w1_raw1", "ts")[c])
-            for k in range(NT // per):
-                rows = slice(per * k, per * (k + 1))
-                acc_e = bank(f"e{c}_{k}", [P, per, width])
-                acc_f = bank(f"f{c}_{k}", [P, per, width])
-                for acc, codes, scales in ((acc_e, w3q, w3s), (acc_f, w4, w4s)):
-                    for i in range(per):
-                        cols = slice((per * k + i) * P, (per * k + i + 1) * P)
-                        nc.tensor.matmul_mx(
-                            out=acc[:, i, :], lhsT=codes[:, cols].bitcast(FP8X4),
-                            lhsT_scale=scales[:, cols], rhs=xq[c][:].bitcast(FP8X4), rhs_scale=xs[c][:],
-                            start=True, stop=True,
-                        )
-                mag = held(f"mag{c}_{k}", [P, per, width], F32, tag="evac", bufs=8)
-                nc.scalar.activation(mag[:], acc_e[:], ACT.Abs)
-                prod = held(f"prod{c}_{k}", [P, per, width], F32, tag=("m1", "m2", "wg0", "wg1", "wg2", "m0")[k % 6])
-                nc.vector.tensor_tensor(prod[:], acc_f[:], mag[:], ALU.mult)
-                unit = j0 * NT // BANK + k
-                (nc.gpsimd if unit in GADD else nc.vector).tensor_tensor(
-                    y[:, rows, :], prod[:],
-                    delay_t[j0 // BANK][:, rows, j0 % BANK : j0 % BANK + width], ALU.add,
-                )
-                if unit in STORES:
-                    first = max([u + 1 for u in STORES if u < unit] + [j0 * NT // BANK]) - j0 * NT // BANK
-                    done = slice(per * first, per * (k + 1))
-                    nc.sync.dma_start(out=out0_rows[:, done, j0 : j0 + width], in_=y[:, done, :])
-
-        for step in ORDER.split():
-            {"f": front, "b": back, "p": planes, "r": lambda c: round_page(PACK - 1, c)}[step[0]](int(step[1]))
+        for c in range(HALVES):
+            round_page(PACK - 1, c)
+        for h in range(HALVES):
+            make_x(h)
+        quantise_page(0)
+        second_products(0)
+        for c in range(HALVES, QUARTERS):
+            round_page(PACK - 1, c)
+        quantise_page(1)
+        for q in range(QUADS):
+            nc.sync.dma_start(
+                out=out_3[0, 4 * q : 4 * q + 4, :].bitcast(I32), in_=page_plane[live_rows(q), :].bitcast(I32)
+            )
+        second_products(1)

from contextlib import ExitStack

import concourse.mybir as mybir
from concourse.masks import make_identity

K, T, S, H, T2, PJ, N = 1024, 4096, 1024, 512, 2048, 1024, 768
FLOPS = 2 * 2 * K * H * S + 2 * 2 * H * N * PJ

F32 = mybir.dt.float32
BF16 = mybir.dt.bfloat16
I32 = mybir.dt.int32
U32 = mybir.dt.uint32
U16 = mybir.dt.uint16
U8 = mybir.dt.uint8
FP8X4 = mybir.dt.float8_e4m3fn_x4
FP4X4 = mybir.dt.float4_e2m1fn_x4
ALU = mybir.AluOpType
ACT = mybir.ActivationFunctionType

P = 128
PACK = 4
K_PASS = P * PACK
PASSES = K // K_PASS
QUADS = 4
PER_COLUMN = 16
BANK = 512
HALVES = 2
N_TILES = N // P
QUARTERS = T2 // BANK
BANKS = {"scalar": 3, "vector": 5}
STAGED = HALVES * PACK - 1


def tile_list_blast_hole_charging_kernel(
    tc, tab_words, tab_scales, offs, offs2, offs3, w1, w2_words, w2_scales, gain, wgs,
    page0, bias, w3, w4_words, w4_scales, delay, out_0, out_1, out_2, out_3,
):
    nc = tc.nc
    with ExitStack() as ctx:
        lists = ctx.enter_context(tc.tile_pool(name="lists", bufs=1))
        keep = ctx.enter_context(tc.tile_pool(name="keep", bufs=1))
        psum = ctx.enter_context(tc.psum_pool(name="psum", bufs=1))

        def held(name, shape, dtype, tag=None, bufs=1):
            return keep.tile(shape, dtype, name=name, tag=tag or name, bufs=bufs, align_bytes=64)

        def bank(name, shape, reader):
            return psum.tile(shape, F32, name=name, tag=reader, bufs=BANKS[reader])

        def half_cols(h):
            return slice(h * BANK, (h + 1) * BANK)

        def entries(list_tile, j0, j1):
            return list_tile[:, j0 // PER_COLUMN : j1 // PER_COLUMN]

        def live_rows(q):
            return slice(32 * q, 32 * q + 4)

        def interleave(copy, dst, src):
            copy(
                dst.rearrange("p (c i t) -> p c t i", i=4, t=PACK),
                src.rearrange("p t (c i) -> p c t i", i=4),
            )

        tab_rows = held("tab_rows", [P, T], U8)
        nc.vector.memset(tab_rows[:].bitcast(I32), 0)
        w2_rows = held("w2_rows", [P, H], U8)
        nc.vector.memset(w2_rows[:].bitcast(I32), 0)
        planes = held("planes", [P, PASSES, S + H], U8)
        nc.vector.memset(planes[:].rearrange("p a c -> p (a c)").bitcast(I32), 0)
        w4_plane = held("w4_plane", [P, N], U8)
        nc.vector.memset(w4_plane[:].bitcast(I32), 0)

        nc.sync.dma_start(
            out=tab_rows[0:P:4, :].bitcast(I32), in_=tab_scales.rearrange("a q t -> q a t").bitcast(I32)
        )
        nc.sync.dma_start(
            out=w2_rows[0:P:4, :].bitcast(I32), in_=w2_scales.rearrange("a q c -> q a c").bitcast(I32)
        )
        ident = held("ident", [P, P], F32)
        make_identity(nc, ident[:])

        offs_t = lists.tile([P, S // PER_COLUMN], U16, name="offs_t")
        nc.sync.dma_start(offs_t[:], offs)
        wgs_t = held("wgs_t", [P, S], F32)
        nc.sync.dma_start(out=wgs_t[:], in_=wgs)
        gain_t = held("gain_t", [P, PACK], F32)
        nc.sync.dma_start(out=gain_t[:], in_=gain.rearrange("(p t) -> p t", t=PACK))
        w2_raw = held("w2_raw", [P, PASSES, 2 * H], U8)
        nc.sync.dma_start(
            out=w2_raw[:].bitcast(I32), in_=w2_words.rearrange("a p c -> p a c").bitcast(I32)
        )
        w1_raw = []
        for a in range(PASSES):
            w1_raw.append(held(f"w1_raw{a}", [P, PACK, H], F32))
            nc.sync.dma_start(
                out=w1_raw[a][:],
                in_=w1[a * K_PASS : (a + 1) * K_PASS, :].rearrange("(p j) c -> p j c", j=PACK),
            )
        offs2_t = lists.tile([P, S // PER_COLUMN], U16, name="offs2_t")
        nc.sync.dma_start(offs2_t[:], offs2)

        page_rows = page0.rearrange("(p t) m -> p t m", t=PACK)
        page = []

        def load_page(t, tag):
            page.append(held(f"page{t}", [P, T2], F32, tag=tag))
            nc.sync.dma_start(out=page[t][:], in_=page_rows[:, t, :])

        tab = []

        def load_tab(a, tag):
            tab.append(held(f"tab{a}", [P, T], I32, tag=tag))
            nc.sync.dma_start(
                out=tab[a][:], in_=tab_words[a].rearrange("p t i -> p (t i)").bitcast(I32)
            )

        wgs_turned = held("wgs_turned", [P, S // P, PACK, P], F32)
        blocks = BANK // P
        for h in range(HALVES):
            turned = bank(f"turned{h}", [P, blocks, P], "scalar")
            for b in range(blocks):
                j0 = h * BANK + b * P
                nc.tensor.transpose(turned[:, b, :], wgs_t[:, j0 : j0 + P], ident[:])
            for q in range(QUADS):
                nc.scalar.copy(
                    wgs_turned[:, blocks * h : blocks * (h + 1), :, 32 * q : 32 * (q + 1)],
                    turned[:].rearrange("j b (p t) -> j b t p", t=PACK),
                )
        load_tab(0, "wgs_t")
        pieces = [(0, 0, BANK), (0, BANK, S)] + [(t, 0, S) for t in range(1, PACK)]
        weight = [held(f"weight{i}", [P, j1 - j0], F32) for i, (t, j0, j1) in enumerate(pieces)]

        def in_piece(tiles, t, h):
            return tiles[h][:] if t == 0 else tiles[t + 1][:, half_cols(h)]

        def make_weight(t):
            for h in range(HALVES):
                back = bank(f"back{t}_{h}", [P, blocks, P], "vector")
                for b in range(blocks):
                    nc.tensor.transpose(back[:, b, :], wgs_turned[:, blocks * h + b, t, :], ident[:])
                nc.scalar.activation(
                    in_piece(weight, t, h), back[:].rearrange("p b j -> p (b j)"), ACT.Copy,
                    scale=gain_t[:, t : t + 1],
                )

        make_weight(0)

        offs3_t = lists.tile([P, PJ // PER_COLUMN], U16, name="offs3_t")
        nc.sync.dma_start(offs3_t[:], offs3)
        bias_t = held("bias_t", [P, PACK], F32)
        nc.gpsimd.dma_start(out=bias_t[:], in_=bias.rearrange("(p t) -> p t", t=PACK))
        for q in range(QUADS):
            nc.gpsimd.dma_start(
                out=w4_plane[live_rows(q), :].bitcast(I32),
                in_=w4_scales[0, 4 * q : 4 * q + 4, :].bitcast(I32),
            )

        w2_codes = held("w2_codes", [P, PASSES, PACK, 2 * P], U8)
        w1_codes, w1_plane = [], []
        for a in range(PASSES):
            nc.vector.tensor_copy(
                w2_codes[:, a, :, :].rearrange("p t (m b) -> p t m b", b=2),
                w2_raw[:, a, :].rearrange("p (m t b) -> p t m b", t=PACK, b=2),
            )
            grouped = held(f"w1_grouped{a}", [P, PACK * H], BF16)
            nc.vector.tensor_copy(
                grouped[:].rearrange("p (t m j) -> p m t j", t=PACK, j=PACK),
                w1_raw[a][:].rearrange("p j (m t) -> p m t j", t=PACK),
            )
            w1_codes.append(held(f"w1_codes{a}", [P, H], U32))
            w1_plane.append(held(f"w1_plane{a}", [P, H], U8))
            nc.vector.quantize_mx(out=w1_codes[a][:].bitcast(FP8X4), scales=w1_plane[a][:], in_=grouped[:])

        load_tab(1, "w2_raw")

        picked_scales = held("picked_scales", [P, S], U8, tag="w1_raw1")
        nc.vector.tensor_copy(picked_scales[:], tab_rows[:].indirect(offs_t[:]))
        scale_rows = held("scale_rows", [P, S + H], U8, tag="w1_grouped0")
        nc.vector.tensor_copy(
            scale_rows[:, S:].rearrange("p (t m) -> p t m", t=PACK),
            w2_rows[:].rearrange("p (m t) -> p t m", t=PACK),
        )
        nc.vector.tensor_copy(scale_rows[:, :S].bitcast(I32), picked_scales[:].bitcast(I32))
        for q in range(QUADS):
            nc.sync.dma_start(
                out=planes[live_rows(q), :, :].bitcast(I32),
                in_=scale_rows[32 * q : 32 * (q + 1) : 4, :].bitcast(I32),
            )

        load_page(0, "w1_raw1")
        for t in range(1, PACK):
            make_weight(t)

        v_codes = {}
        for a in range(PASSES):
            for h in range(HALVES):
                v_codes[a, h] = held(f"v_codes{a}_{h}", [P, BANK], U32)
                nc.vector.tensor_copy(
                    v_codes[a, h][:],
                    tab[a][:].bitcast(U32).indirect(entries(offs_t, h * BANK, (h + 1) * BANK)),
                )

        w3_raw = held("w3_raw", [P, PACK, N], F32, tag="wgs_t")
        nc.sync.dma_start(out=w3_raw[:], in_=w3.rearrange("(p j) c -> p j c", j=PACK))
        load_page(1, "w2_raw")

        largest = []

        def first_products(t, h):
            cols = slice(t * P, (t + 1) * P)
            acc_a = bank(f"a{t}_{h}", [P, BANK], "scalar")
            acc_b = bank(f"b{t}_{h}", [P, BANK], "vector")
            for a in range(PASSES):
                moving = dict(
                    rhs=v_codes[a, h][:].bitcast(FP8X4), rhs_scale=planes[:, a, half_cols(h)],
                    start=(a == 0), stop=(a == PASSES - 1),
                )
                nc.tensor.matmul_mx(
                    out=acc_a[:], lhsT=w1_codes[a][:, cols].bitcast(FP8X4),
                    lhsT_scale=w1_plane[a][:, cols], **moving,
                )
                nc.tensor.matmul_mx(
                    out=acc_b[:], lhsT=w2_codes[:, a, t, :].bitcast(FP4X4),
                    lhsT_scale=planes[:, a, S + t * P : S + (t + 1) * P], **moving,
                )
            if (t, h) == (0, 1):
                a_sb = held("a_sb0_1", [P, BANK], F32)
            else:
                a_sb = held(f"a_sb{t}_{h}", [P, BANK], F32, tag="staged", bufs=STAGED)
            nc.scalar.copy(a_sb[:], acc_a[:])
            nc.vector.tensor_tensor(in_piece(largest, t, h), acc_b[:], a_sb[:], ALU.max)

        def put(i):
            t, j0, j1 = pieces[i]
            nc.vector.tensor_tensor(
                page[t][:].indirect(entries(offs2_t, j0, j1)), largest[i][:], weight[i][:], ALU.mult
            )

        w3_codes = held("w3_codes", [P, N], U32)
        w3_plane = held("w3_plane", [P, N], U8)

        def quantise_w3():
            w3_grouped = held("w3_grouped", [P, PACK * N], BF16, tag="a_sb0_1")
            for c0, c1 in ((0, BANK), (BANK, N)):
                interleave(nc.scalar.copy, w3_grouped[:, PACK * c0 : PACK * c1], w3_raw[:, :, c0:c1])
                nc.vector.quantize_mx(
                    out=w3_codes[:, c0:c1].bitcast(FP8X4), scales=w3_plane[:, c0:c1],
                    in_=w3_grouped[:, PACK * c0 : PACK * c1],
                )

        out1_rows = out_1.rearrange("(p t) m -> p t m", t=PACK)
        largest_tags = ("largest0", "largest0", "weight0", "weight1", "largest4")
        page_tags = {1: "largest0", 2: "weight0"}
        for i, (t, j0, j1) in enumerate(pieces):
            largest.append(held(f"largest{i}", [P, j1 - j0], F32, tag=largest_tags[i]))
            for h in range(j0 // BANK, j1 // BANK):
                first_products(t, h)
            put(i)
            if j1 == S:
                nc.sync.dma_start(out=out1_rows[:, t, :], in_=page[t][:])
            if i in page_tags:
                load_page(i + 1, page_tags[i])
            if i == 2:
                quantise_w3()

        page_grouped = [
            held(f"page_grouped{c}", [P, BANK, PACK], BF16, tag=f"v_codes{c // HALVES}_{c % HALVES}")
            for c in range(QUARTERS)
        ]

        def round_page(t, c):
            nc.scalar.copy(page_grouped[c][:, :, t], page[t][:, c * BANK : (c + 1) * BANK])

        for t in range(PACK - 1):
            for c in range(QUARTERS):
                round_page(t, c)

        w4_codes = held("w4_codes", [P, N], I32, tag="wgs_t")
        nc.sync.dma_start(out=w4_codes[:], in_=w4_words[0].rearrange("p n i -> p (n i)").bitcast(I32))
        delay_rows = delay.rearrange("(b p) j -> p b j", p=P)
        delay_t = []
        for h, tag in enumerate(("a_sb0_1", "w2_codes")):
            delay_t.append(held(f"delay{h}", [P, N_TILES, BANK], F32, tag=tag))
            nc.sync.dma_start(out=delay_t[h][:], in_=delay_rows[:, :, half_cols(h)])

        out0_rows = out_0.rearrange("(b p) j -> p b j", p=P)
        out2_words = out_2[0].rearrange("p m i -> p (m i)").bitcast(I32)
        page_plane = held("page_plane", [P, T2], U8)
        x_codes, x_plane = [], []

        def make_x(h):
            picked = held(f"picked{h}", [P, PACK, BANK], F32, tag=("weight4", "largest4")[h])
            rounded = held(f"rounded{h}", [P, PACK, BANK], BF16)
            for t in range(PACK):
                nc.vector.tensor_copy(
                    picked[:, t, :], page[t][:].indirect(entries(offs3_t, h * BANK, (h + 1) * BANK))
                )
                nc.scalar.activation(
                    rounded[:, t, :], picked[:, t, :], ACT.Identity, bias=bias_t[:, t : t + 1]
                )
            x_grouped = held(f"x_grouped{h}", [P, PACK * BANK], BF16)
            interleave((nc.scalar.copy, nc.vector.tensor_copy)[h], x_grouped[:], rounded[:])
            x_codes.append(held(f"x_codes{h}", [P, BANK], U32))
            x_plane.append(held(f"x_plane{h}", [P, BANK], U8))
            nc.vector.quantize_mx(out=x_codes[h][:].bitcast(FP8X4), scales=x_plane[h][:], in_=x_grouped[:])

        def quantise_page(h):
            page_codes = held(f"page_codes{h}", [P, HALVES * BANK], U32, tag=f"x_grouped{h}")
            for i in range(HALVES):
                c = HALVES * h + i
                nc.vector.quantize_mx(
                    out=page_codes[:, half_cols(i)].bitcast(FP8X4),
                    scales=page_plane[:, c * BANK : (c + 1) * BANK],
                    in_=page_grouped[c][:].rearrange("p m t -> p (m t)"),
                )
            nc.sync.dma_start(
                out=out2_words[:, HALVES * h * BANK : HALVES * (h + 1) * BANK], in_=page_codes[:].bitcast(I32)
            )

        product_tags = ("weight1", "weight2", "weight3", "tab_rows", "w1_raw0", "w1_grouped1")

        def second_products(h):
            y = held(f"y{h}", [P, N_TILES, BANK], F32, tag=("wgs_turned", "w1_grouped0")[h])
            for k in range(N_TILES):
                cols = slice(k * P, (k + 1) * P)
                acc_e = bank(f"e{h}_{k}", [P, BANK], "scalar")
                acc_f = bank(f"f{h}_{k}", [P, BANK], "vector")
                for acc, codes, plane in ((acc_e, w3_codes, w3_plane), (acc_f, w4_codes, w4_plane)):
                    nc.tensor.matmul_mx(
                        out=acc[:], lhsT=codes[:, cols].bitcast(FP8X4), lhsT_scale=plane[:, cols],
                        rhs=x_codes[h][:].bitcast(FP8X4), rhs_scale=x_plane[h][:], start=True, stop=True,
                    )
                size = held(f"size{h}_{k}", [P, BANK], F32, tag="staged", bufs=STAGED)
                nc.scalar.activation(size[:], acc_e[:], ACT.Abs)
                product = held(f"product{h}_{k}", [P, BANK], F32, tag=product_tags[k])
                nc.vector.tensor_tensor(product[:], acc_f[:], size[:], ALU.mult)
                last = h == HALVES - 1 and k == N_TILES - 1
                adder = nc.gpsimd if k % 2 == 1 and not last else nc.vector
                adder.tensor_tensor(y[:, k, :], product[:], delay_t[h][:, k, :], ALU.add)
                nc.sync.dma_start(out=out0_rows[:, k, half_cols(h)], in_=y[:, k, :])

        for c in range(HALVES):
            round_page(PACK - 1, c)
        for h in range(HALVES):
            make_x(h)
        quantise_page(0)
        second_products(0)
        for c in range(HALVES, QUARTERS):
            round_page(PACK - 1, c)
        quantise_page(1)
        for q in range(QUADS):
            nc.sync.dma_start(
                out=out_3[0, 4 * q : 4 * q + 4, :].bitcast(I32), in_=page_plane[live_rows(q), :].bitcast(I32)
            )
        second_products(1)
